import numpy as np
import ml_dtypes


def mxq(x, axis, fmt="e4m3"):
    dtype, down = {"e4m3": (ml_dtypes.float8_e4m3fn, 7), "e5m2": (ml_dtypes.float8_e5m2, 14)}[fmt]
    v = np.moveaxis(np.asarray(x, np.float32).astype(ml_dtypes.bfloat16).astype(np.float64), axis, -1)
    blocks = v.reshape(v.shape[:-1] + (-1, 32))
    amax = np.abs(blocks).max(-1, keepdims=True)
    byte = np.maximum(np.where(amax > 0, np.frexp(amax)[1] - 1 + 127, 0) - down, 1)
    scale = np.exp2(byte - 127.0)
    codes = (blocks / scale).astype(np.float32).astype(dtype).astype(np.float64)
    return np.moveaxis((codes * scale).reshape(v.shape), -1, axis)


WIDE = False


def mx_kscale(k):
    if not WIDE:
        return np.ones(k)
    levels = np.array([30, -30])
    if k % 512:
        return np.exp2(np.random.permutation(np.resize(levels, k // 32))).repeat(32)
    a = np.empty((k // 512, 16))
    for p in range(k // 512):
        a[p, :8] = np.random.permutation(np.resize(levels, 8))
        for g in range(8):
            far = levels[np.abs(levels - a[p, g]) >= 10]
            a[p, g + 8] = far[np.random.randint(len(far))]
    return np.exp2(a.ravel()).repeat(32)


def f64(x):
    return np.asarray(x).astype(np.float64)


def striped(idx):
    return np.tile(np.asarray(idx).reshape(-1, 16).T, (8, 1)).astype(np.uint16)


def unstriped(offs):
    return offs[:16].T.reshape(-1).astype(np.int64)


E2M1 = np.array([0.0, 0.5, 1.0, 1.5, 2.0, 3.0, 4.0, 6.0, -0.0, -0.5, -1.0, -1.5, -2.0, -3.0, -4.0, -6.0])


def pack_weight(w, fmt):
    k, n = w.shape
    w = f64(np.asarray(w, np.float32).astype(ml_dtypes.bfloat16)).reshape(k // 32, 32, n)
    amax = np.abs(w).max(1)
    if fmt in ("e4m3", "e5m2"):
        byte = np.frexp(amax)[1] - 1 + 127 - (7 if fmt == "e4m3" else 14)
    else:
        mant, ex = np.frexp(amax / 6.0)
        byte = np.where(mant > 0.5, ex, ex - 1) + 127
    byte = np.clip(np.where(amax > 0, byte, 1), 1, 254)
    scaled = (w * np.exp2(127.0 - byte)[:, None, :]).reshape(k, n).astype(np.float32)
    by_word = np.ascontiguousarray(scaled.reshape(k // 512, 128, 4, n).transpose(0, 1, 3, 2))
    if fmt in ("e4m3", "e5m2"):
        words = by_word.astype(ml_dtypes.float8_e4m3fn if fmt == "e4m3" else ml_dtypes.float8_e5m2).view(np.uint8)
    else:
        c = by_word.astype(ml_dtypes.float4_e2m1fn).view(np.uint8) & 0xF
        words = (c[..., 0::2] | (c[..., 1::2] << 4)).reshape(k // 512, 128, 2 * n)
    return np.ascontiguousarray(words), np.ascontiguousarray(byte.astype(np.uint8).reshape(k // 512, 16, n))


def unpack_weight(words, scales, fmt):
    g, _, n = scales.shape
    words = np.ascontiguousarray(words).reshape(g, 128, n, -1)
    if fmt in ("e4m3", "e5m2"):
        vals = words.view(ml_dtypes.float8_e4m3fn if fmt == "e4m3" else ml_dtypes.float8_e5m2).astype(np.float64)
    else:
        nib = np.empty((g, 128, n, 4), np.uint8)
        nib[..., 0::2] = words & 0xF
        nib[..., 1::2] = words >> 4
        vals = E2M1[nib]
    vals = vals * np.repeat(np.exp2(scales.astype(np.float64) - 127.0), 8, axis=1)[..., None]
    return vals.transpose(0, 1, 3, 2).reshape(g * 512, n)


def sigmoid(v):
    return 1.0 / (1.0 + np.exp(-v))


K, T, J, S, R, F, Z, N = 512, 512, 256, 512, 512, 512, 1024, 256


def setup_inputs():
    n = np.random.standard_normal
    idx = np.random.permutation(T)[:J]
    idx2 = np.random.permutation(S)[:J]
    idx3 = np.random.permutation(Z)[:J]
    fk = mx_kscale(K)
    fr = mx_kscale(R)
    ff = mx_kscale(F)
    wp = pack_weight(n((K, R)) * 1 / np.sqrt(K) * fk[:, None] * fr, "e2m1")
    w2p = pack_weight(n((F, R)) * 1 / np.sqrt(F) * ff[:, None] * fr, "e5m2")
    wbp = pack_weight(n((R, N)) * 1 / np.sqrt(R) / fr[:, None], "e5m2")
    return {
        "xa": (n((K, T))).astype(np.float32),
        "xb": (n((K, S))).astype(np.float32),
        "fk": (np.random.uniform(0.5, 2.0, (K, 1)) / fk[:, None]).astype(np.float32),
        "w_words": wp[0],
        "w_scales": wp[1],
        "xo": (n((F, Z))).astype(np.float32),
        "fl": (np.random.uniform(0.5, 2.0, (F, 1)) / ff[:, None]).astype(np.float32),
        "so": (n((F, J))).astype(np.float32),
        "w2_words": w2p[0],
        "w2_scales": w2p[1],
        "wb_words": wbp[0],
        "wb_scales": wbp[1],
        "rs": (n((N, J))).astype(np.float32),
        "offs": striped(idx),
        "offs2": striped(idx2),
        "offs3": striped(idx3),
    }


def reference(xa, xb, fk, w_words, w_scales, xo, fl, so, w2_words, w2_scales, wb_words, wb_scales, rs, offs, offs2, offs3):
    idx = unstriped(offs)
    idx2 = unstriped(offs2)
    idx3 = unstriped(offs3)
    wu = unpack_weight(w_words, w_scales, "e2m1")
    w2u = unpack_weight(w2_words, w2_scales, "e5m2")
    wbu = unpack_weight(wb_words, wb_scales, "e5m2")
    u = f64(xa)[:, idx] * f64(xb)[:, idx2] * f64(fk)
    u2 = f64(xo)[:, idx3] * sigmoid(f64(so)) * f64(fl)
    uq = mxq(u, 0, "e4m3")
    a = wu.T @ uq
    u2q = mxq(u2, 0, "e5m2")
    q = w2u.T @ u2q
    hid = np.abs(a - q)
    hidq = mxq(hid, 0, "e5m2")
    p = wbu.T @ hidq
    p1 = np.pad(p, ((0, 0), (1, 0)))[:, :J]
    y = p - 0.7 * p1 + 0.5 * f64(rs)
    return y

@@ -1,0 +1,216 @@
+from contextlib import ExitStack
+
+import concourse.mybir as mybir
+
+K, T, J, S, R, F, Z, N = 512, 512, 256, 512, 512, 512, 1024, 256
+FLOPS = 2 * K * R * J + 2 * F * R * J + 2 * R * N * J
+
+F32 = mybir.dt.float32
+BF16 = mybir.dt.bfloat16
+I32 = mybir.dt.int32
+U32 = mybir.dt.uint32
+U16 = mybir.dt.uint16
+U8 = mybir.dt.uint8
+E4M3X4 = mybir.dt.float8_e4m3fn_x4
+E5M2X4 = mybir.dt.float8_e5m2_x4
+E2M1X4 = mybir.dt.float4_e2m1fn_x4
+MULT = mybir.AluOpType.mult
+ADD = mybir.AluOpType.add
+ACT = mybir.ActivationFunctionType
+
+P = 128
+PACK = 4
+HALF = J // 2
+LAG = 0.7
+
+
+def tile_list_two_entryproducts_gated_absgap_lagged_kernel(
+    tc, xa, xb, fk, w_words, w_scales, xo, fl, so, w2_words, w2_scales, wb_words, wb_scales, rs, offs, offs2, offs3, out
+):
+    nc = tc.nc
+
+    with ExitStack() as ctx:
+        sb = ctx.enter_context(tc.tile_pool(name="sb", bufs=1))
+        psum = ctx.enter_context(tc.psum_pool(name="psum", bufs=1))
+
+        def tile(name, shape, dtype):
+            return sb.tile(shape, dtype, name=name, align_bytes=64)
+
+        list_a = tile("list_a", [P, J // 16], U16)
+        list_b = tile("list_b", [P, J // 16], U16)
+        list_o = tile("list_o", [P, J // 16], U16)
+        gates = tile("gates", [P, PACK * J], F32)
+        table_a = tile("table_a", [P, PACK * T], F32)
+        table_b = tile("table_b", [P, PACK * S], F32)
+        table_o = [tile("table_o%d" % t, [P, Z], F32) for t in range(PACK)]
+        fk_sb = tile("fk_sb", [P, PACK], F32)
+        fl_sb = tile("fl_sb", [P, PACK], F32)
+        w_raw = tile("w_raw", [P, 2 * R], U8)
+        w2_raw = tile("w2_raw", [P, R], U32)
+        wb_codes = tile("wb_codes", [P, N], U32)
+        w_raw_scales = tile("w_raw_scales", [P, R], U8)
+        w2_raw_scales = tile("w2_raw_scales", [P, R], U8)
+        wb_plane = tile("wb_plane", [P, N], U8)
+        resid = tile("resid", [P, N // P, J], F32)
+
+        for plane in (w_raw_scales, w2_raw_scales, wb_plane):
+            nc.vector.memset(plane[:].bitcast(U32), 0)
+
+        def load_scale_rows(engine, plane, scales, quadrant):
+            engine.dma_start(
+                out=plane[32 * quadrant : 32 * quadrant + 4, :].bitcast(I32),
+                in_=scales[0, 4 * quadrant : 4 * quadrant + 4, :].bitcast(I32),
+            )
+
+        def rows_by_partition(x):
+            return x.rearrange("(p t) c -> p (t c)", t=PACK)
+
+        xo_planes = xo.rearrange("(p t) c -> t p c", t=PACK)
+
+        nc.gpsimd.dma_start(out=fl_sb[:], in_=rows_by_partition(fl))
+        nc.gpsimd.dma_start(out=fk_sb[:], in_=rows_by_partition(fk))
+        for quadrant in range(4):
+            load_scale_rows(nc.gpsimd, w2_raw_scales, w2_scales, quadrant)
+
+        nc.sync.dma_start(out=gates[:], in_=rows_by_partition(so))
+        nc.sync.dma_start(out=table_a[:], in_=rows_by_partition(xa))
+        nc.sync.dma_start(list_a[:], offs)
+        nc.sync.dma_start(list_b[:], offs2)
+        for quadrant in range(3):
+            load_scale_rows(nc.sync, w_raw_scales, w_scales, quadrant)
+        nc.sync.dma_start(out=table_b[:], in_=rows_by_partition(xb))
+        load_scale_rows(nc.sync, w_raw_scales, w_scales, 3)
+        nc.sync.dma_start(out=w_raw[:].bitcast(I32), in_=w_words[0].bitcast(I32))
+        nc.sync.dma_start(out=w2_raw[:].bitcast(I32), in_=w2_words[0].rearrange("p n t -> p (n t)").bitcast(I32))
+        nc.sync.dma_start(out=table_o[0][:], in_=xo_planes[0])
+        nc.sync.dma_start(list_o[:], offs3)
+        for t in range(1, PACK):
+            nc.sync.dma_start(out=table_o[t][:], in_=xo_planes[t])
+        nc.sync.dma_start(out=wb_codes[:].bitcast(I32), in_=wb_words[0].rearrange("p n t -> p (n t)").bitcast(I32))
+        for quadrant in range(4):
+            load_scale_rows(nc.sync, wb_plane, wb_scales, quadrant)
+        nc.sync.dma_start(out=resid[:], in_=rs.rearrange("(c p) j -> p c j", p=P))
+
+        sig = tile("sig", [P, PACK * J], F32)
+        gain = tile("gain", [P, PACK * J], F32)
+        nc.scalar.activation(sig[:], gates[:], ACT.Sigmoid)
+        for t in range(PACK):
+            cols = slice(t * J, (t + 1) * J)
+            nc.vector.tensor_scalar(gain[:, cols], sig[:, cols], fl_sb[:, t : t + 1], -1.0, MULT, MULT)
+
+        picked_a = tile("picked_a", [P, PACK * J], F32)
+        picked_b = tile("picked_b", [P, PACK * J], F32)
+        u = tile("u", [P, PACK, J], F32)
+        for t in range(PACK):
+            nc.scalar.activation(
+                picked_a[:, t * J : (t + 1) * J], table_a[:, t * T : (t + 1) * T].indirect(list_a[:]), ACT.Copy
+            )
+        for t in range(PACK):
+            cols = slice(t * J, (t + 1) * J)
+            nc.scalar.activation(picked_b[:, cols], table_b[:, t * S : (t + 1) * S].indirect(list_b[:]), ACT.Copy)
+            nc.vector.scalar_tensor_tensor(
+                u[:, t, :], picked_a[:, cols], fk_sb[:, t : t + 1], picked_b[:, cols], MULT, MULT
+            )
+        u_bf = tile("u_bf", [P, J, PACK], BF16)
+        nc.scalar.copy(
+            u_bf[:].rearrange("p (c i) t -> p c t i", i=4), u[:].rearrange("p t (c i) -> p c t i", i=4)
+        )
+        u_codes = tile("u_codes", [P, J], U32)
+        u_plane = tile("u_plane", [P, J], U8)
+        nc.vector.quantize_mx(u_codes[:].bitcast(E4M3X4), u_plane[:], u_bf[:].rearrange("p j t -> p (j t)"))
+
+        w_codes = tile("w_codes", [P, 2 * R], U8)
+        w2_codes = tile("w2_codes", [P, R], U32)
+        w_plane = tile("w_plane", [P, R], U8)
+        w2_plane = tile("w2_plane", [P, R], U8)
+        nc.vector.tensor_copy(
+            w_codes[:].bitcast(U16).rearrange("p (t c i) -> p c t i", t=PACK, i=8),
+            w_raw[:].bitcast(U16).rearrange("p (c i t) -> p c t i", t=PACK, i=8),
+        )
+        nc.vector.tensor_copy(
+            w2_codes[:].rearrange("p (t c i) -> p c t i", t=PACK, i=4),
+            w2_raw[:].rearrange("p (c i t) -> p c t i", t=PACK, i=4),
+        )
+        for dealt, raw in ((w_plane, w_raw_scales), (w2_plane, w2_raw_scales)):
+            nc.vector.tensor_copy(
+                dealt[:].rearrange("p (t q) -> p t q", t=PACK), raw[:].rearrange("p (q t) -> p t q", t=PACK)
+            )
+
+        gap = [psum.tile([P, PACK, HALF], F32, name="gap%d" % h) for h in range(2)]
+        prod = [psum.tile([P, N // P, HALF], F32, name="prod%d" % h) for h in range(2)]
+        for h in range(2):
+            slots = slice(h * HALF, (h + 1) * HALF)
+            for t in range(PACK):
+                nc.tensor.matmul_mx(
+                    gap[h][:, t, :],
+                    lhsT=w_codes[:, 2 * P * t : 2 * P * (t + 1)].bitcast(E2M1X4),
+                    lhsT_scale=w_plane[:, P * t : P * (t + 1)],
+                    rhs=u_codes[:, slots].bitcast(E4M3X4),
+                    rhs_scale=u_plane[:, slots],
+                    start=(t == 0),
+                    stop=False,
+                )
+
+        u2 = tile("u2", [P, PACK, J], F32)
+        for t in range(PACK - 1):
+            nc.vector.tensor_tensor(u2[:, t, :], table_o[t][:].indirect(list_o[:]), gain[:, t * J : (t + 1) * J], MULT)
+
+        last = PACK - 1
+        for h in range(2):
+            slots = slice(h * HALF, (h + 1) * HALF)
+            nc.vector.tensor_tensor(
+                u2[:, last, slots],
+                table_o[last][:].indirect(list_o[:, h * HALF // 16 : (h + 1) * HALF // 16]),
+                gain[:, last * J + h * HALF : last * J + (h + 1) * HALF],
+                MULT,
+            )
+            u2_bf = tile("u2_bf%d" % h, [P, HALF, PACK], BF16)
+            nc.vector.tensor_copy(
+                u2_bf[:].rearrange("p (c i) t -> p c t i", i=4),
+                u2[:, :, slots].rearrange("p t (c i) -> p c t i", i=4),
+            )
+            u2_codes = tile("u2_codes%d" % h, [P, HALF], U32)
+            u2_plane = tile("u2_plane%d" % h, [P, HALF], U8)
+            nc.vector.quantize_mx(u2_codes[:].bitcast(E5M2X4), u2_plane[:], u2_bf[:].rearrange("p j t -> p (j t)"))
+            for t in range(PACK):
+                nc.tensor.matmul_mx(
+                    gap[h][:, t, :],
+                    lhsT=w2_codes[:, P * t : P * (t + 1)].bitcast(E5M2X4),
+                    lhsT_scale=w2_plane[:, P * t : P * (t + 1)],
+                    rhs=u2_codes[:].bitcast(E5M2X4),
+                    rhs_scale=u2_plane[:],
+                    start=False,
+                    stop=(t == PACK - 1),
+                )
+
+        out_rows = out.rearrange("(c p) j -> p c j", p=P)
+        for h in range(2):
+            slots = slice(h * HALF, (h + 1) * HALF)
+            hid_bf = tile("hid_bf%d" % h, [P, HALF, PACK], BF16)
+            nc.scalar.activation(hid_bf[:], gap[h][:].rearrange("p t j -> p j t"), ACT.Abs)
+            hid_codes = tile("hid_codes%d" % h, [P, HALF], U32)
+            hid_plane = tile("hid_plane%d" % h, [P, HALF], U8)
+            nc.vector.quantize_mx(hid_codes[:].bitcast(E5M2X4), hid_plane[:], hid_bf[:].rearrange("p j t -> p (j t)"))
+            for c in range(N // P):
+                nc.tensor.matmul_mx(
+                    prod[h][:, c, :],
+                    lhsT=wb_codes[:, P * c : P * (c + 1)].bitcast(E5M2X4),
+                    lhsT_scale=wb_plane[:, P * c : P * (c + 1)],
+                    rhs=hid_codes[:].bitcast(E5M2X4),
+                    rhs_scale=hid_plane[:],
+                    start=True,
+                    stop=True,
+                )
+            first = h * HALF + 1
+            count = min(HALF, J - first)
+            nc.vector.scalar_tensor_tensor(
+                resid[:, :, first : first + count],
+                prod[h][:, :, 0:count],
+                -2.0 * LAG,
+                resid[:, :, first : first + count],
+                MULT,
+                ADD,
+            )
+            result = tile("result%d" % h, [P, N // P, HALF], F32)
+            nc.vector.scalar_tensor_tensor(result[:], resid[:, :, slots], 0.5, prod[h][:], MULT, ADD)
+            nc.sync.dma_start(out=out_rows[:, :, slots], in_=result[:])

@@ -33,15 +33,15 @@ def tile_list_two_entryproducts_gated_absgap_lagged_kernel(
         sb = ctx.enter_context(tc.tile_pool(name="sb", bufs=1))
         psum = ctx.enter_context(tc.psum_pool(name="psum", bufs=1))
 
-        def tile(name, shape, dtype):
-            return sb.tile(shape, dtype, name=name, align_bytes=64)
+        def tile(name, shape, dtype, tag=None):
+            return sb.tile(shape, dtype, name=name, tag=tag or name, align_bytes=64)
 
         list_a = tile("list_a", [P, J // 16], U16)
         list_b = tile("list_b", [P, J // 16], U16)
         list_o = tile("list_o", [P, J // 16], U16)
         gates = tile("gates", [P, PACK * J], F32)
         table_a = tile("table_a", [P, PACK * T], F32)
-        table_b = tile("table_b", [P, PACK * S], F32)
+        table_b = [tile("table_b%d" % i, [P, 2 * S], F32) for i in range(2)]
         table_o = [tile("table_o%d" % t, [P, Z], F32) for t in range(PACK)]
         fk_sb = tile("fk_sb", [P, PACK], F32)
         fl_sb = tile("fl_sb", [P, PACK], F32)
@@ -67,47 +67,60 @@ def tile_list_two_entryproducts_gated_absgap_lagged_kernel(
 
         xo_planes = xo.rearrange("(p t) c -> t p c", t=PACK)
 
-        nc.gpsimd.dma_start(out=fl_sb[:], in_=rows_by_partition(fl))
-        nc.gpsimd.dma_start(out=fk_sb[:], in_=rows_by_partition(fk))
-        for quadrant in range(4):
-            load_scale_rows(nc.gpsimd, w2_raw_scales, w2_scales, quadrant)
-
+        xb_rows = rows_by_partition(xb)
         nc.sync.dma_start(out=gates[:], in_=rows_by_partition(so))
+        nc.sync.dma_start(out=fl_sb[:], in_=rows_by_partition(fl))
+        load_scale_rows(nc.sync, w_raw_scales, w_scales, 0)
+        nc.sync.dma_start(out=w_raw[:].bitcast(I32), in_=w_words[0].bitcast(I32))
+        load_scale_rows(nc.sync, w_raw_scales, w_scales, 1)
         nc.sync.dma_start(out=table_a[:], in_=rows_by_partition(xa))
         nc.sync.dma_start(list_a[:], offs)
-        nc.sync.dma_start(list_b[:], offs2)
-        for quadrant in range(3):
-            load_scale_rows(nc.sync, w_raw_scales, w_scales, quadrant)
-        nc.sync.dma_start(out=table_b[:], in_=rows_by_partition(xb))
+        load_scale_rows(nc.sync, w_raw_scales, w_scales, 2)
+        nc.sync.dma_start(out=table_b[0][:], in_=xb_rows[:, 0 : 2 * S])
         load_scale_rows(nc.sync, w_raw_scales, w_scales, 3)
-        nc.sync.dma_start(out=w_raw[:].bitcast(I32), in_=w_words[0].bitcast(I32))
-        nc.sync.dma_start(out=w2_raw[:].bitcast(I32), in_=w2_words[0].rearrange("p n t -> p (n t)").bitcast(I32))
+        nc.sync.dma_start(list_b[:], offs2)
+        nc.sync.dma_start(out=table_b[1][:], in_=xb_rows[:, 2 * S : 4 * S])
+        nc.sync.dma_start(out=fk_sb[:], in_=rows_by_partition(fk))
+        for quadrant in range(2):
+            load_scale_rows(nc.sync, w2_raw_scales, w2_scales, quadrant)
         nc.sync.dma_start(out=table_o[0][:], in_=xo_planes[0])
+        load_scale_rows(nc.sync, w2_raw_scales, w2_scales, 2)
         nc.sync.dma_start(list_o[:], offs3)
-        for t in range(1, PACK):
+        nc.sync.dma_start(out=table_o[1][:], in_=xo_planes[1])
+        load_scale_rows(nc.sync, w2_raw_scales, w2_scales, 3)
+        for t in range(2, PACK):
             nc.sync.dma_start(out=table_o[t][:], in_=xo_planes[t])
+        nc.sync.dma_start(out=w2_raw[:].bitcast(I32), in_=w2_words[0].rearrange("p n t -> p (n t)").bitcast(I32))
         nc.sync.dma_start(out=wb_codes[:].bitcast(I32), in_=wb_words[0].rearrange("p n t -> p (n t)").bitcast(I32))
+        nc.sync.dma_start(out=resid[:], in_=rs.rearrange("(c p) j -> p c j", p=P))
         for quadrant in range(4):
             load_scale_rows(nc.sync, wb_plane, wb_scales, quadrant)
-        nc.sync.dma_start(out=resid[:], in_=rs.rearrange("(c p) j -> p c j", p=P))
 
         sig = tile("sig", [P, PACK * J], F32)
-        gain = tile("gain", [P, PACK * J], F32)
+        gain = [tile("gain%d" % t, [P, J], F32) for t in range(PACK)]
         nc.scalar.activation(sig[:], gates[:], ACT.Sigmoid)
         for t in range(PACK):
             cols = slice(t * J, (t + 1) * J)
-            nc.vector.tensor_scalar(gain[:, cols], sig[:, cols], fl_sb[:, t : t + 1], -1.0, MULT, MULT)
+            nc.vector.tensor_scalar(gain[t][:], sig[:, cols], fl_sb[:, t : t + 1], -1.0, MULT, MULT)
 
         picked_a = tile("picked_a", [P, PACK * J], F32)
         picked_b = tile("picked_b", [P, PACK * J], F32)
         u = tile("u", [P, PACK, J], F32)
         for t in range(PACK):
-            nc.scalar.activation(
-                picked_a[:, t * J : (t + 1) * J], table_a[:, t * T : (t + 1) * T].indirect(list_a[:]), ACT.Copy
-            )
+            window = table_a[:, t * T : (t + 1) * T].indirect(list_a[:])
+            if t < 1:
+                nc.scalar.activation(picked_a[:, t * J : (t + 1) * J], window, ACT.Copy)
+            else:
+                nc.vector.tensor_copy(picked_a[:, t * J : (t + 1) * J], window)
         for t in range(PACK):
             cols = slice(t * J, (t + 1) * J)
-            nc.scalar.activation(picked_b[:, cols], table_b[:, t * S : (t + 1) * S].indirect(list_b[:]), ACT.Copy)
+            window = table_b[t // 2][:, t % 2 * S : (t % 2 + 1) * S].indirect(list_b[:])
+            if t < 3:
+                nc.scalar.activation(picked_b[:, cols], window, ACT.Copy)
+            else:
+                nc.vector.tensor_copy(picked_b[:, cols], window)
+        for t in (0, 1, 3, 2):
+            cols = slice(t * J, (t + 1) * J)
             nc.vector.scalar_tensor_tensor(
                 u[:, t, :], picked_a[:, cols], fk_sb[:, t : t + 1], picked_b[:, cols], MULT, MULT
             )
@@ -115,26 +128,30 @@ def tile_list_two_entryproducts_gated_absgap_lagged_kernel(
         nc.scalar.copy(
             u_bf[:].rearrange("p (c i) t -> p c t i", i=4), u[:].rearrange("p t (c i) -> p c t i", i=4)
         )
-        u_codes = tile("u_codes", [P, J], U32)
-        u_plane = tile("u_plane", [P, J], U8)
-        nc.vector.quantize_mx(u_codes[:].bitcast(E4M3X4), u_plane[:], u_bf[:].rearrange("p j t -> p (j t)"))
-
         w_codes = tile("w_codes", [P, 2 * R], U8)
-        w2_codes = tile("w2_codes", [P, R], U32)
         w_plane = tile("w_plane", [P, R], U8)
-        w2_plane = tile("w2_plane", [P, R], U8)
         nc.vector.tensor_copy(
             w_codes[:].bitcast(U16).rearrange("p (t c i) -> p c t i", t=PACK, i=8),
             w_raw[:].bitcast(U16).rearrange("p (c i t) -> p c t i", t=PACK, i=8),
         )
-        nc.vector.tensor_copy(
-            w2_codes[:].rearrange("p (t c i) -> p c t i", t=PACK, i=4),
-            w2_raw[:].rearrange("p (c i t) -> p c t i", t=PACK, i=4),
-        )
-        for dealt, raw in ((w_plane, w_raw_scales), (w2_plane, w2_raw_scales)):
+        def deal_scales(dealt, raw):
             nc.vector.tensor_copy(
                 dealt[:].rearrange("p (t q) -> p t q", t=PACK), raw[:].rearrange("p (q t) -> p t q", t=PACK)
             )
+
+        deal_scales(w_plane, w_raw_scales)
+
+        u2 = tile("u2", [P, PACK, J], F32, tag="picked_b")
+        for t in range(2):
+            nc.vector.tensor_tensor(u2[:, t, :], table_o[t][:].indirect(list_o[:]), gain[t][:], MULT)
+        w2_plane = tile("w2_plane", [P, R], U8, tag="gain0")
+        deal_scales(w2_plane, w2_raw_scales)
+        picked_o2 = tile("picked_o2", [P, J], F32)
+        nc.scalar.activation(picked_o2[:], table_o[2][:].indirect(list_o[:]), ACT.Copy)
+        nc.vector.tensor_tensor(u2[:, 2, :], picked_o2[:], gain[2][:], MULT)
+        u_codes = tile("u_codes", [P, J], U32, tag="gain1")
+        u_plane = tile("u_plane", [P, J], U8)
+        nc.vector.quantize_mx(u_codes[:].bitcast(E4M3X4), u_plane[:], u_bf[:].rearrange("p j t -> p (j t)"))
 
         gap = [psum.tile([P, PACK, HALF], F32, name="gap%d" % h) for h in range(2)]
         prod = [psum.tile([P, N // P, HALF], F32, name="prod%d" % h) for h in range(2)]
@@ -151,25 +168,31 @@ def tile_list_two_entryproducts_gated_absgap_lagged_kernel(
                     stop=False,
                 )
 
-        u2 = tile("u2", [P, PACK, J], F32)
-        for t in range(PACK - 1):
-            nc.vector.tensor_tensor(u2[:, t, :], table_o[t][:].indirect(list_o[:]), gain[:, t * J : (t + 1) * J], MULT)
 
         last = PACK - 1
         for h in range(2):
             slots = slice(h * HALF, (h + 1) * HALF)
-            nc.vector.tensor_tensor(
-                u2[:, last, slots],
-                table_o[last][:].indirect(list_o[:, h * HALF // 16 : (h + 1) * HALF // 16]),
-                gain[:, last * J + h * HALF : last * J + (h + 1) * HALF],
-                MULT,
-            )
+            window = table_o[last][:].indirect(list_o[:, h * HALF // 16 : (h + 1) * HALF // 16])
+            if h == 0:
+                nc.vector.tensor_tensor(u2[:, last, slots], window, gain[last][:, slots], MULT)
+            else:
+                picked_o = tile("picked_o", [P, HALF], F32)
+                nc.scalar.activation(picked_o[:], window, ACT.Copy)
+                nc.vector.tensor_tensor(u2[:, last, slots], picked_o[:], gain[last][:, slots], MULT)
+        w2_codes = tile("w2_codes", [P, R], U32, tag="gain3")
+        nc.vector.tensor_copy(
+            w2_codes[:].rearrange("p (t c i) -> p c t i", t=PACK, i=4),
+            w2_raw[:].rearrange("p (c i t) -> p c t i", t=PACK, i=4),
+        )
+        for h in range(2):
+            slots = slice(h * HALF, (h + 1) * HALF)
             u2_bf = tile("u2_bf%d" % h, [P, HALF, PACK], BF16)
-            nc.vector.tensor_copy(
+            interleave = nc.vector.tensor_copy if h == 0 else nc.scalar.copy
+            interleave(
                 u2_bf[:].rearrange("p (c i) t -> p c t i", i=4),
                 u2[:, :, slots].rearrange("p t (c i) -> p c t i", i=4),
             )
-            u2_codes = tile("u2_codes%d" % h, [P, HALF], U32)
+            u2_codes = tile("u2_codes%d" % h, [P, HALF], U32, tag="picked_o" if h == 0 else None)
             u2_plane = tile("u2_plane%d" % h, [P, HALF], U8)
             nc.vector.quantize_mx(u2_codes[:].bitcast(E5M2X4), u2_plane[:], u2_bf[:].rearrange("p j t -> p (j t)"))
             for t in range(PACK):
@@ -203,14 +226,14 @@ def tile_list_two_entryproducts_gated_absgap_lagged_kernel(
                 )
             first = h * HALF + 1
             count = min(HALF, J - first)
-            nc.vector.scalar_tensor_tensor(
-                resid[:, :, first : first + count],
-                prod[h][:, :, 0:count],
-                -2.0 * LAG,
-                resid[:, :, first : first + count],
-                MULT,
-                ADD,
-            )
-            result = tile("result%d" % h, [P, N // P, HALF], F32)
-            nc.vector.scalar_tensor_tensor(result[:], resid[:, :, slots], 0.5, prod[h][:], MULT, ADD)
-            nc.sync.dma_start(out=out_rows[:, :, slots], in_=result[:])
+            ahead = slice(first, first + count)
+            pieces = [slice(0, 2)] if h == 0 else [slice(0, 1), slice(1, 2)]
+            for c in pieces:
+                nc.vector.scalar_tensor_tensor(
+                    resid[:, c, ahead], prod[h][:, c, 0:count], -2.0 * LAG, resid[:, c, ahead], MULT, ADD
+                )
+            for c in pieces:
+                result = tile("result%d_%d" % (h, c.start), [P, c.stop - c.start, HALF], F32)
+                nc.vector.scalar_tensor_tensor(result[:], resid[:, c, slots], 0.5, prod[h][:, c, :], MULT, ADD)
+                queue = nc.sync if c.start == 0 else nc.scalar
+                queue.dma_start(out=out_rows[:, c, slots], in_=result[:])

@@ -53,8 +53,9 @@ def tile_list_two_entryproducts_gated_absgap_lagged_kernel(
         wb_plane = tile("wb_plane", [P, N], U8)
         resid = tile("resid", [P, N // P, J], F32)
 
-        for plane in (w_raw_scales, w2_raw_scales, wb_plane):
-            nc.vector.memset(plane[:].bitcast(U32), 0)
+        for plane in (w_raw_scales, w2_raw_scales):
+            nc.gpsimd.memset(plane[:].bitcast(U32), 0)
+        nc.vector.memset(wb_plane[:].bitcast(U32), 0)
 
         def load_scale_rows(engine, plane, scales, quadrant):
             engine.dma_start(
@@ -68,27 +69,20 @@ def tile_list_two_entryproducts_gated_absgap_lagged_kernel(
         xo_planes = xo.rearrange("(p t) c -> t p c", t=PACK)
 
         xb_rows = rows_by_partition(xb)
-        nc.sync.dma_start(out=gates[:], in_=rows_by_partition(so))
-        nc.sync.dma_start(out=fl_sb[:], in_=rows_by_partition(fl))
-        load_scale_rows(nc.sync, w_raw_scales, w_scales, 0)
-        nc.sync.dma_start(out=w_raw[:].bitcast(I32), in_=w_words[0].bitcast(I32))
-        load_scale_rows(nc.sync, w_raw_scales, w_scales, 1)
-        nc.sync.dma_start(out=table_a[:], in_=rows_by_partition(xa))
+        for plane, scales in ((w_raw_scales, w_scales), (w2_raw_scales, w2_scales)):
+            for quadrant in range(4):
+                load_scale_rows(nc.gpsimd, plane, scales, quadrant)
+        nc.scalar.dma_start(out=gates[:], in_=rows_by_partition(so))
         nc.sync.dma_start(list_a[:], offs)
-        load_scale_rows(nc.sync, w_raw_scales, w_scales, 2)
-        nc.sync.dma_start(out=table_b[0][:], in_=xb_rows[:, 0 : 2 * S])
-        load_scale_rows(nc.sync, w_raw_scales, w_scales, 3)
         nc.sync.dma_start(list_b[:], offs2)
-        nc.sync.dma_start(out=table_b[1][:], in_=xb_rows[:, 2 * S : 4 * S])
-        nc.sync.dma_start(out=fk_sb[:], in_=rows_by_partition(fk))
-        for quadrant in range(2):
-            load_scale_rows(nc.sync, w2_raw_scales, w2_scales, quadrant)
-        nc.sync.dma_start(out=table_o[0][:], in_=xo_planes[0])
-        load_scale_rows(nc.sync, w2_raw_scales, w2_scales, 2)
         nc.sync.dma_start(list_o[:], offs3)
-        nc.sync.dma_start(out=table_o[1][:], in_=xo_planes[1])
-        load_scale_rows(nc.sync, w2_raw_scales, w2_scales, 3)
-        for t in range(2, PACK):
+        nc.sync.dma_start(out=fl_sb[:], in_=rows_by_partition(fl))
+        nc.sync.dma_start(out=fk_sb[:], in_=rows_by_partition(fk))
+        nc.sync.dma_start(out=w_raw[:].bitcast(I32), in_=w_words[0].bitcast(I32))
+        nc.sync.dma_start(out=table_a[:], in_=rows_by_partition(xa))
+        for i in range(2):
+            nc.sync.dma_start(out=table_b[i][:], in_=xb_rows[:, 2 * S * i : 2 * S * (i + 1)])
+        for t in range(PACK):
             nc.sync.dma_start(out=table_o[t][:], in_=xo_planes[t])
         nc.sync.dma_start(out=w2_raw[:].bitcast(I32), in_=w2_words[0].rearrange("p n t -> p (n t)").bitcast(I32))
         nc.sync.dma_start(out=wb_codes[:].bitcast(I32), in_=wb_words[0].rearrange("p n t -> p (n t)").bitcast(I32))
@@ -129,7 +123,7 @@ def tile_list_two_entryproducts_gated_absgap_lagged_kernel(
             u_bf[:].rearrange("p (c i) t -> p c t i", i=4), u[:].rearrange("p t (c i) -> p c t i", i=4)
         )
         w_codes = tile("w_codes", [P, 2 * R], U8)
-        w_plane = tile("w_plane", [P, R], U8)
+        w_plane = tile("w_plane", [P, R], U8, tag="table_a")
         nc.vector.tensor_copy(
             w_codes[:].bitcast(U16).rearrange("p (t c i) -> p c t i", t=PACK, i=8),
             w_raw[:].bitcast(U16).rearrange("p (c i t) -> p c t i", t=PACK, i=8),

@@ -86,9 +86,9 @@ def tile_list_two_entryproducts_gated_absgap_lagged_kernel(
             nc.sync.dma_start(out=table_o[t][:], in_=xo_planes[t])
         nc.sync.dma_start(out=w2_raw[:].bitcast(I32), in_=w2_words[0].rearrange("p n t -> p (n t)").bitcast(I32))
         nc.sync.dma_start(out=wb_codes[:].bitcast(I32), in_=wb_words[0].rearrange("p n t -> p (n t)").bitcast(I32))
-        nc.sync.dma_start(out=resid[:], in_=rs.rearrange("(c p) j -> p c j", p=P))
         for quadrant in range(4):
             load_scale_rows(nc.sync, wb_plane, wb_scales, quadrant)
+        nc.sync.dma_start(out=resid[:], in_=rs.rearrange("(c p) j -> p c j", p=P))
 
         sig = tile("sig", [P, PACK * J], F32)
         gain = [tile("gain%d" % t, [P, J], F32) for t in range(PACK)]
@@ -138,7 +138,7 @@ def tile_list_two_entryproducts_gated_absgap_lagged_kernel(
         u2 = tile("u2", [P, PACK, J], F32, tag="picked_b")
         for t in range(2):
             nc.vector.tensor_tensor(u2[:, t, :], table_o[t][:].indirect(list_o[:]), gain[t][:], MULT)
-        w2_plane = tile("w2_plane", [P, R], U8, tag="gain0")
+        w2_plane = tile("w2_plane", [P, R], U8, tag="table_o1")
         deal_scales(w2_plane, w2_raw_scales)
         picked_o2 = tile("picked_o2", [P, J], F32)
         nc.scalar.activation(picked_o2[:], table_o[2][:].indirect(list_o[:]), ACT.Copy)

@@ -53,9 +53,9 @@ def tile_list_two_entryproducts_gated_absgap_lagged_kernel(
         wb_plane = tile("wb_plane", [P, N], U8)
         resid = tile("resid", [P, N // P, J], F32)
 
-        for plane in (w_raw_scales, w2_raw_scales):
-            nc.gpsimd.memset(plane[:].bitcast(U32), 0)
-        nc.vector.memset(wb_plane[:].bitcast(U32), 0)
+        nc.gpsimd.memset(w2_raw_scales[:].bitcast(U32), 0)
+        for plane in (w_raw_scales, wb_plane):
+            nc.vector.memset(plane[:].bitcast(U32), 0)
 
         def load_scale_rows(engine, plane, scales, quadrant):
             engine.dma_start(
@@ -69,9 +69,8 @@ def tile_list_two_entryproducts_gated_absgap_lagged_kernel(
         xo_planes = xo.rearrange("(p t) c -> t p c", t=PACK)
 
         xb_rows = rows_by_partition(xb)
-        for plane, scales in ((w_raw_scales, w_scales), (w2_raw_scales, w2_scales)):
-            for quadrant in range(4):
-                load_scale_rows(nc.gpsimd, plane, scales, quadrant)
+        for quadrant in range(4):
+            load_scale_rows(nc.gpsimd, w2_raw_scales, w2_scales, quadrant)
         nc.scalar.dma_start(out=gates[:], in_=rows_by_partition(so))
         nc.sync.dma_start(list_a[:], offs)
         nc.sync.dma_start(list_b[:], offs2)
@@ -80,6 +79,8 @@ def tile_list_two_entryproducts_gated_absgap_lagged_kernel(
         nc.sync.dma_start(out=fk_sb[:], in_=rows_by_partition(fk))
         nc.sync.dma_start(out=w_raw[:].bitcast(I32), in_=w_words[0].bitcast(I32))
         nc.sync.dma_start(out=table_a[:], in_=rows_by_partition(xa))
+        for quadrant in range(4):
+            load_scale_rows(nc.sync, w_raw_scales, w_scales, quadrant)
         for i in range(2):
             nc.sync.dma_start(out=table_b[i][:], in_=xb_rows[:, 2 * S * i : 2 * S * (i + 1)])
         for t in range(PACK):
@@ -102,19 +103,14 @@ def tile_list_two_entryproducts_gated_absgap_lagged_kernel(
         u = tile("u", [P, PACK, J], F32)
         for t in range(PACK):
             window = table_a[:, t * T : (t + 1) * T].indirect(list_a[:])
-            if t < 1:
+            if t < 2:
                 nc.scalar.activation(picked_a[:, t * J : (t + 1) * J], window, ACT.Copy)
             else:
                 nc.vector.tensor_copy(picked_a[:, t * J : (t + 1) * J], window)
         for t in range(PACK):
             cols = slice(t * J, (t + 1) * J)
             window = table_b[t // 2][:, t % 2 * S : (t % 2 + 1) * S].indirect(list_b[:])
-            if t < 3:
-                nc.scalar.activation(picked_b[:, cols], window, ACT.Copy)
-            else:
-                nc.vector.tensor_copy(picked_b[:, cols], window)
-        for t in (0, 1, 3, 2):
-            cols = slice(t * J, (t + 1) * J)
+            nc.scalar.activation(picked_b[:, cols], window, ACT.Copy)
             nc.vector.scalar_tensor_tensor(
                 u[:, t, :], picked_a[:, cols], fk_sb[:, t : t + 1], picked_b[:, cols], MULT, MULT
             )
@@ -123,7 +119,7 @@ def tile_list_two_entryproducts_gated_absgap_lagged_kernel(
             u_bf[:].rearrange("p (c i) t -> p c t i", i=4), u[:].rearrange("p t (c i) -> p c t i", i=4)
         )
         w_codes = tile("w_codes", [P, 2 * R], U8)
-        w_plane = tile("w_plane", [P, R], U8, tag="table_a")
+        w_plane = tile("w_plane", [P, R], U8)
         nc.vector.tensor_copy(
             w_codes[:].bitcast(U16).rearrange("p (t c i) -> p c t i", t=PACK, i=8),
             w_raw[:].bitcast(U16).rearrange("p (c i t) -> p c t i", t=PACK, i=8),
@@ -134,12 +130,12 @@ def tile_list_two_entryproducts_gated_absgap_lagged_kernel(
             )
 
         deal_scales(w_plane, w_raw_scales)
+        w2_plane = tile("w2_plane", [P, R], U8, tag="table_a")
+        deal_scales(w2_plane, w2_raw_scales)
 
         u2 = tile("u2", [P, PACK, J], F32, tag="picked_b")
         for t in range(2):
             nc.vector.tensor_tensor(u2[:, t, :], table_o[t][:].indirect(list_o[:]), gain[t][:], MULT)
-        w2_plane = tile("w2_plane", [P, R], U8, tag="table_o1")
-        deal_scales(w2_plane, w2_raw_scales)
         picked_o2 = tile("picked_o2", [P, J], F32)
         nc.scalar.activation(picked_o2[:], table_o[2][:].indirect(list_o[:]), ACT.Copy)
         nc.vector.tensor_tensor(u2[:, 2, :], picked_o2[:], gain[2][:], MULT)
@@ -148,7 +144,6 @@ def tile_list_two_entryproducts_gated_absgap_lagged_kernel(
         nc.vector.quantize_mx(u_codes[:].bitcast(E4M3X4), u_plane[:], u_bf[:].rearrange("p j t -> p (j t)"))
 
         gap = [psum.tile([P, PACK, HALF], F32, name="gap%d" % h) for h in range(2)]
-        prod = [psum.tile([P, N // P, HALF], F32, name="prod%d" % h) for h in range(2)]
         for h in range(2):
             slots = slice(h * HALF, (h + 1) * HALF)
             for t in range(PACK):
@@ -208,26 +203,29 @@ def tile_list_two_entryproducts_gated_absgap_lagged_kernel(
             hid_codes = tile("hid_codes%d" % h, [P, HALF], U32)
             hid_plane = tile("hid_plane%d" % h, [P, HALF], U8)
             nc.vector.quantize_mx(hid_codes[:].bitcast(E5M2X4), hid_plane[:], hid_bf[:].rearrange("p j t -> p (j t)"))
-            for c in range(N // P):
-                nc.tensor.matmul_mx(
-                    prod[h][:, c, :],
-                    lhsT=wb_codes[:, P * c : P * (c + 1)].bitcast(E5M2X4),
-                    lhsT_scale=wb_plane[:, P * c : P * (c + 1)],
-                    rhs=hid_codes[:].bitcast(E5M2X4),
-                    rhs_scale=hid_plane[:],
-                    start=True,
-                    stop=True,
-                )
             first = h * HALF + 1
             count = min(HALF, J - first)
             ahead = slice(first, first + count)
             pieces = [slice(0, 2)] if h == 0 else [slice(0, 1), slice(1, 2)]
-            for c in pieces:
+            prod = {}
+            for piece in pieces:
+                prod[piece.start] = psum.tile([P, piece.stop - piece.start, HALF], F32, name="prod%d_%d" % (h, piece.start))
+                for c in range(piece.start, piece.stop):
+                    nc.tensor.matmul_mx(
+                        prod[piece.start][:, c - piece.start, :],
+                        lhsT=wb_codes[:, P * c : P * (c + 1)].bitcast(E5M2X4),
+                        lhsT_scale=wb_plane[:, P * c : P * (c + 1)],
+                        rhs=hid_codes[:].bitcast(E5M2X4),
+                        rhs_scale=hid_plane[:],
+                        start=True,
+                        stop=True,
+                    )
+            for piece in pieces:
                 nc.vector.scalar_tensor_tensor(
-                    resid[:, c, ahead], prod[h][:, c, 0:count], -2.0 * LAG, resid[:, c, ahead], MULT, ADD
+                    resid[:, piece, ahead], prod[piece.start][:, :, 0:count], -2.0 * LAG, resid[:, piece, ahead], MULT, ADD
                 )
-            for c in pieces:
-                result = tile("result%d_%d" % (h, c.start), [P, c.stop - c.start, HALF], F32)
-                nc.vector.scalar_tensor_tensor(result[:], resid[:, c, slots], 0.5, prod[h][:, c, :], MULT, ADD)
-                queue = nc.sync if c.start == 0 else nc.scalar
-                queue.dma_start(out=out_rows[:, c, slots], in_=result[:])
+            for piece in pieces:
+                result = tile("result%d_%d" % (h, piece.start), [P, piece.stop - piece.start, HALF], F32)
+                nc.vector.scalar_tensor_tensor(result[:], resid[:, piece, slots], 0.5, prod[piece.start][:], MULT, ADD)
+                queue = nc.sync if piece.start == 0 else nc.scalar
+                queue.dma_start(out=out_rows[:, piece, slots], in_=result[:])

from contextlib import ExitStack

import concourse.mybir as mybir

K, T, J, S, R, F, Z, N = 512, 512, 256, 512, 512, 512, 1024, 256
FLOPS = 2 * K * R * J + 2 * F * R * J + 2 * R * N * J

F32 = mybir.dt.float32
BF16 = mybir.dt.bfloat16
I32 = mybir.dt.int32
U32 = mybir.dt.uint32
U16 = mybir.dt.uint16
U8 = mybir.dt.uint8
E4M3X4 = mybir.dt.float8_e4m3fn_x4
E5M2X4 = mybir.dt.float8_e5m2_x4
E2M1X4 = mybir.dt.float4_e2m1fn_x4
MULT = mybir.AluOpType.mult
ADD = mybir.AluOpType.add
ACT = mybir.ActivationFunctionType

P = 128
PACK = 4
HALF = J // 2
LAG = 0.7


def tile_list_two_entryproducts_gated_absgap_lagged_kernel(
    tc, xa, xb, fk, w_words, w_scales, xo, fl, so, w2_words, w2_scales, wb_words, wb_scales, rs, offs, offs2, offs3, out
):
    nc = tc.nc

    with ExitStack() as ctx:
        sb = ctx.enter_context(tc.tile_pool(name="sb", bufs=1))
        psum = ctx.enter_context(tc.psum_pool(name="psum", bufs=1))

        def tile(name, shape, dtype, tag=None):
            return sb.tile(shape, dtype, name=name, tag=tag or name, align_bytes=64)

        list_a = tile("list_a", [P, J // 16], U16)
        list_b = tile("list_b", [P, J // 16], U16)
        list_o = tile("list_o", [P, J // 16], U16)
        gates = tile("gates", [P, PACK * J], F32)
        table_a = tile("table_a", [P, PACK * T], F32)
        table_b = [tile("table_b%d" % i, [P, 2 * S], F32) for i in range(2)]
        table_o = [tile("table_o%d" % t, [P, Z], F32) for t in range(PACK)]
        fk_sb = tile("fk_sb", [P, PACK], F32)
        fl_sb = tile("fl_sb", [P, PACK], F32)
        w_raw = tile("w_raw", [P, 2 * R], U8)
        w2_raw = tile("w2_raw", [P, R], U32)
        wb_codes = tile("wb_codes", [P, N], U32)
        w_raw_scales = tile("w_raw_scales", [P, R], U8)
        w2_raw_scales = tile("w2_raw_scales", [P, R], U8)
        wb_plane = tile("wb_plane", [P, N], U8)
        resid = tile("resid", [P, N // P, J], F32)

        nc.gpsimd.memset(w2_raw_scales[:].bitcast(U32), 0)
        for plane in (w_raw_scales, wb_plane):
            nc.vector.memset(plane[:].bitcast(U32), 0)

        def load_scale_rows(engine, plane, scales, quadrant):
            engine.dma_start(
                out=plane[32 * quadrant : 32 * quadrant + 4, :].bitcast(I32),
                in_=scales[0, 4 * quadrant : 4 * quadrant + 4, :].bitcast(I32),
            )

        def rows_by_partition(x):
            return x.rearrange("(p t) c -> p (t c)", t=PACK)

        xo_planes = xo.rearrange("(p t) c -> t p c", t=PACK)

        xb_rows = rows_by_partition(xb)
        for quadrant in range(4):
            load_scale_rows(nc.gpsimd, w2_raw_scales, w2_scales, quadrant)
        nc.scalar.dma_start(out=gates[:], in_=rows_by_partition(so))
        nc.sync.dma_start(list_a[:], offs)
        nc.sync.dma_start(list_b[:], offs2)
        nc.sync.dma_start(list_o[:], offs3)
        nc.sync.dma_start(out=fl_sb[:], in_=rows_by_partition(fl))
        nc.sync.dma_start(out=fk_sb[:], in_=rows_by_partition(fk))
        nc.sync.dma_start(out=w_raw[:].bitcast(I32), in_=w_words[0].bitcast(I32))
        nc.sync.dma_start(out=table_a[:], in_=rows_by_partition(xa))
        for quadrant in range(4):
            load_scale_rows(nc.sync, w_raw_scales, w_scales, quadrant)
        for i in range(2):
            nc.sync.dma_start(out=table_b[i][:], in_=xb_rows[:, 2 * S * i : 2 * S * (i + 1)])
        for t in range(PACK):
            nc.sync.dma_start(out=table_o[t][:], in_=xo_planes[t])
        nc.sync.dma_start(out=w2_raw[:].bitcast(I32), in_=w2_words[0].rearrange("p n t -> p (n t)").bitcast(I32))
        nc.sync.dma_start(out=wb_codes[:].bitcast(I32), in_=wb_words[0].rearrange("p n t -> p (n t)").bitcast(I32))
        for quadrant in range(4):
            load_scale_rows(nc.sync, wb_plane, wb_scales, quadrant)
        nc.sync.dma_start(out=resid[:], in_=rs.rearrange("(c p) j -> p c j", p=P))

        sig = tile("sig", [P, PACK * J], F32)
        gain = [tile("gain%d" % t, [P, J], F32) for t in range(PACK)]
        nc.scalar.activation(sig[:], gates[:], ACT.Sigmoid)
        for t in range(PACK):
            cols = slice(t * J, (t + 1) * J)
            nc.vector.tensor_scalar(gain[t][:], sig[:, cols], fl_sb[:, t : t + 1], -1.0, MULT, MULT)

        picked_a = tile("picked_a", [P, PACK * J], F32)
        picked_b = tile("picked_b", [P, PACK * J], F32)
        u = tile("u", [P, PACK, J], F32)
        for t in range(PACK):
            window = table_a[:, t * T : (t + 1) * T].indirect(list_a[:])
            if t < 2:
                nc.scalar.activation(picked_a[:, t * J : (t + 1) * J], window, ACT.Copy)
            else:
                nc.vector.tensor_copy(picked_a[:, t * J : (t + 1) * J], window)
        for t in range(PACK):
            cols = slice(t * J, (t + 1) * J)
            window = table_b[t // 2][:, t % 2 * S : (t % 2 + 1) * S].indirect(list_b[:])
            nc.scalar.activation(picked_b[:, cols], window, ACT.Copy)
            nc.vector.scalar_tensor_tensor(
                u[:, t, :], picked_a[:, cols], fk_sb[:, t : t + 1], picked_b[:, cols], MULT, MULT
            )
        u_bf = tile("u_bf", [P, J, PACK], BF16)
        nc.scalar.copy(
            u_bf[:].rearrange("p (c i) t -> p c t i", i=4), u[:].rearrange("p t (c i) -> p c t i", i=4)
        )
        w_codes = tile("w_codes", [P, 2 * R], U8)
        w_plane = tile("w_plane", [P, R], U8)
        nc.vector.tensor_copy(
            w_codes[:].bitcast(U16).rearrange("p (t c i) -> p c t i", t=PACK, i=8),
            w_raw[:].bitcast(U16).rearrange("p (c i t) -> p c t i", t=PACK, i=8),
        )
        def deal_scales(dealt, raw):
            nc.vector.tensor_copy(
                dealt[:].rearrange("p (t q) -> p t q", t=PACK), raw[:].rearrange("p (q t) -> p t q", t=PACK)
            )

        deal_scales(w_plane, w_raw_scales)
        w2_plane = tile("w2_plane", [P, R], U8, tag="table_a")
        deal_scales(w2_plane, w2_raw_scales)

        u2 = tile("u2", [P, PACK, J], F32, tag="picked_b")
        for t in range(2):
            nc.vector.tensor_tensor(u2[:, t, :], table_o[t][:].indirect(list_o[:]), gain[t][:], MULT)
        picked_o2 = tile("picked_o2", [P, J], F32)
        nc.scalar.activation(picked_o2[:], table_o[2][:].indirect(list_o[:]), ACT.Copy)
        nc.vector.tensor_tensor(u2[:, 2, :], picked_o2[:], gain[2][:], MULT)
        u_codes = tile("u_codes", [P, J], U32, tag="gain1")
        u_plane = tile("u_plane", [P, J], U8)
        nc.vector.quantize_mx(u_codes[:].bitcast(E4M3X4), u_plane[:], u_bf[:].rearrange("p j t -> p (j t)"))

        gap = [psum.tile([P, PACK, HALF], F32, name="gap%d" % h) for h in range(2)]
        for h in range(2):
            slots = slice(h * HALF, (h + 1) * HALF)
            for t in range(PACK):
                nc.tensor.matmul_mx(
                    gap[h][:, t, :],
                    lhsT=w_codes[:, 2 * P * t : 2 * P * (t + 1)].bitcast(E2M1X4),
                    lhsT_scale=w_plane[:, P * t : P * (t + 1)],
                    rhs=u_codes[:, slots].bitcast(E4M3X4),
                    rhs_scale=u_plane[:, slots],
                    start=(t == 0),
                    stop=False,
                )


        last = PACK - 1
        for h in range(2):
            slots = slice(h * HALF, (h + 1) * HALF)
            window = table_o[last][:].indirect(list_o[:, h * HALF // 16 : (h + 1) * HALF // 16])
            if h == 0:
                nc.vector.tensor_tensor(u2[:, last, slots], window, gain[last][:, slots], MULT)
            else:
                picked_o = tile("picked_o", [P, HALF], F32)
                nc.scalar.activation(picked_o[:], window, ACT.Copy)
                nc.vector.tensor_tensor(u2[:, last, slots], picked_o[:], gain[last][:, slots], MULT)
        w2_codes = tile("w2_codes", [P, R], U32, tag="gain3")
        nc.vector.tensor_copy(
            w2_codes[:].rearrange("p (t c i) -> p c t i", t=PACK, i=4),
            w2_raw[:].rearrange("p (c i t) -> p c t i", t=PACK, i=4),
        )
        for h in range(2):
            slots = slice(h * HALF, (h + 1) * HALF)
            u2_bf = tile("u2_bf%d" % h, [P, HALF, PACK], BF16)
            interleave = nc.vector.tensor_copy if h == 0 else nc.scalar.copy
            interleave(
                u2_bf[:].rearrange("p (c i) t -> p c t i", i=4),
                u2[:, :, slots].rearrange("p t (c i) -> p c t i", i=4),
            )
            u2_codes = tile("u2_codes%d" % h, [P, HALF], U32, tag="picked_o" if h == 0 else None)
            u2_plane = tile("u2_plane%d" % h, [P, HALF], U8)
            nc.vector.quantize_mx(u2_codes[:].bitcast(E5M2X4), u2_plane[:], u2_bf[:].rearrange("p j t -> p (j t)"))
            for t in range(PACK):
                nc.tensor.matmul_mx(
                    gap[h][:, t, :],
                    lhsT=w2_codes[:, P * t : P * (t + 1)].bitcast(E5M2X4),
                    lhsT_scale=w2_plane[:, P * t : P * (t + 1)],
                    rhs=u2_codes[:].bitcast(E5M2X4),
                    rhs_scale=u2_plane[:],
                    start=False,
                    stop=(t == PACK - 1),
                )

        out_rows = out.rearrange("(c p) j -> p c j", p=P)
        for h in range(2):
            slots = slice(h * HALF, (h + 1) * HALF)
            hid_bf = tile("hid_bf%d" % h, [P, HALF, PACK], BF16)
            nc.scalar.activation(hid_bf[:], gap[h][:].rearrange("p t j -> p j t"), ACT.Abs)
            hid_codes = tile("hid_codes%d" % h, [P, HALF], U32)
            hid_plane = tile("hid_plane%d" % h, [P, HALF], U8)
            nc.vector.quantize_mx(hid_codes[:].bitcast(E5M2X4), hid_plane[:], hid_bf[:].rearrange("p j t -> p (j t)"))
            first = h * HALF + 1
            count = min(HALF, J - first)
            ahead = slice(first, first + count)
            pieces = [slice(0, 2)] if h == 0 else [slice(0, 1), slice(1, 2)]
            prod = {}
            for piece in pieces:
                prod[piece.start] = psum.tile([P, piece.stop - piece.start, HALF], F32, name="prod%d_%d" % (h, piece.start))
                for c in range(piece.start, piece.stop):
                    nc.tensor.matmul_mx(
                        prod[piece.start][:, c - piece.start, :],
                        lhsT=wb_codes[:, P * c : P * (c + 1)].bitcast(E5M2X4),
                        lhsT_scale=wb_plane[:, P * c : P * (c + 1)],
                        rhs=hid_codes[:].bitcast(E5M2X4),
                        rhs_scale=hid_plane[:],
                        start=True,
                        stop=True,
                    )
            for piece in pieces:
                nc.vector.scalar_tensor_tensor(
                    resid[:, piece, ahead], prod[piece.start][:, :, 0:count], -2.0 * LAG, resid[:, piece, ahead], MULT, ADD
                )
            for piece in pieces:
                result = tile("result%d_%d" % (h, piece.start), [P, piece.stop - piece.start, HALF], F32)
                nc.vector.scalar_tensor_tensor(result[:], resid[:, piece, slots], 0.5, prod[piece.start][:], MULT, ADD)
                queue = nc.sync if piece.start == 0 else nc.scalar
                queue.dma_start(out=out_rows[:, piece, slots], in_=result[:])
